import numpy as np
import ml_dtypes


def mxq(x, axis, fmt="e4m3"):
    dtype, down = {"e4m3": (ml_dtypes.float8_e4m3fn, 7), "e5m2": (ml_dtypes.float8_e5m2, 14)}[fmt]
    v = np.moveaxis(np.asarray(x, np.float32).astype(ml_dtypes.bfloat16).astype(np.float64), axis, -1)
    blocks = v.reshape(v.shape[:-1] + (-1, 32))
    amax = np.abs(blocks).max(-1, keepdims=True)
    byte = np.maximum(np.where(amax > 0, np.frexp(amax)[1] - 1 + 127, 0) - down, 1)
    scale = np.exp2(byte - 127.0)
    codes = (blocks / scale).astype(np.float32).astype(dtype).astype(np.float64)
    return np.moveaxis((codes * scale).reshape(v.shape), -1, axis)


WIDE = False


def mx_kscale(k):
    if not WIDE:
        return np.ones(k)
    levels = np.array([10, -10, 5, -5, 0])
    if k % 512:
        return np.exp2(np.random.permutation(np.resize(levels, k // 32))).repeat(32)
    a = np.empty((k // 512, 16))
    for p in range(k // 512):
        a[p, :8] = np.random.permutation(np.resize(levels, 8))
        for g in range(8):
            far = levels[np.abs(levels - a[p, g]) >= 10]
            a[p, g + 8] = far[np.random.randint(len(far))]
    return np.exp2(a.ravel()).repeat(32)


def f64(x):
    return np.asarray(x).astype(np.float64)


def striped8(idx):
    return np.asarray(idx).reshape(8, -1, 16).transpose(0, 2, 1).reshape(128, -1).astype(np.uint16)


def unstriped8(offs):
    return offs.reshape(8, 16, -1).transpose(0, 2, 1).reshape(8, -1).astype(np.int64)


def pick8(x, idx, run):
    r = np.arange(len(x))
    return x[r[:, None], idx[r % (8 * run) // run]]


E2M1 = np.array([0.0, 0.5, 1.0, 1.5, 2.0, 3.0, 4.0, 6.0, -0.0, -0.5, -1.0, -1.5, -2.0, -3.0, -4.0, -6.0])


def pack_weight(w, fmt):
    k, n = w.shape
    w = f64(np.asarray(w, np.float32).astype(ml_dtypes.bfloat16)).reshape(k // 32, 32, n)
    amax = np.abs(w).max(1)
    if fmt == "e4m3":
        byte = np.frexp(amax)[1] - 1 + 127 - 7
    else:
        mant, ex = np.frexp(amax / 6.0)
        byte = np.where(mant > 0.5, ex, ex - 1) + 127
    byte = np.clip(np.where(amax > 0, byte, 1), 1, 254)
    scaled = (w * np.exp2(127.0 - byte)[:, None, :]).reshape(k, n).astype(np.float32)
    by_word = np.ascontiguousarray(scaled.reshape(k // 512, 128, 4, n).transpose(0, 1, 3, 2))
    if fmt == "e4m3":
        words = by_word.astype(ml_dtypes.float8_e4m3fn).view(np.uint8)
    else:
        c = by_word.astype(ml_dtypes.float4_e2m1fn).view(np.uint8) & 0xF
        words = (c[..., 0::2] | (c[..., 1::2] << 4)).reshape(k // 512, 128, 2 * n)
    return np.ascontiguousarray(words), np.ascontiguousarray(byte.astype(np.uint8).reshape(k // 512, 16, n))


def unpack_weight(words, scales, fmt):
    g, _, n = scales.shape
    words = np.ascontiguousarray(words).reshape(g, 128, n, -1)
    if fmt == "e4m3":
        vals = words.view(ml_dtypes.float8_e4m3fn).astype(np.float64)
    else:
        nib = np.empty((g, 128, n, 4), np.uint8)
        nib[..., 0::2] = words & 0xF
        nib[..., 1::2] = words >> 4
        vals = E2M1[nib]
    vals = vals * np.repeat(np.exp2(scales.astype(np.float64) - 127.0), 8, axis=1)[..., None]
    return vals.transpose(0, 1, 3, 2).reshape(g * 512, n)


def sigmoid(v):
    return 1.0 / (1.0 + np.exp(-v))


D, T, U, I, Q = 512, 1024, 1024, 512, 128


def setup_inputs():
    n = np.random.standard_normal
    idx = np.stack([np.random.permutation(T)[:I] for _ in range(8)])
    idx2 = np.stack([np.random.permutation(U)[:I] for _ in range(8)])
    idx3 = np.stack([np.random.permutation(T)[:I] for _ in range(8)])
    idx4 = np.stack([np.random.permutation(T)[:I] for _ in range(8)])
    idx5 = np.stack([np.random.permutation(U)[:I] for _ in range(8)])
    idx6 = np.stack([np.random.permutation(U)[:I] for _ in range(8)])
    fd = mx_kscale(D)
    keysp = pack_weight(n((D, T)) / fd[:, None], "e4m3")
    notesp = pack_weight(n((D, U)) / fd[:, None], "e2m1")
    return {
        "query": (n((D, Q)) * 1.0 / np.sqrt(D) * fd[:, None]).astype(np.float32),
        "keys_words": keysp[0],
        "keys_scales": keysp[1],
        "notes_words": notesp[0],
        "notes_scales": notesp[1],
        "thr": (np.random.uniform(-0.6, 0.6, (Q, 1))).astype(np.float32),
        "slope": (np.random.uniform(1.0, 3.0, (Q, 1))).astype(np.float32),
        "offs": striped8(idx),
        "offs2": striped8(idx2),
        "offs3": striped8(idx3),
        "offs4": striped8(idx4),
        "offs5": striped8(idx5),
        "offs6": striped8(idx6),
    }


def reference(query, keys_words, keys_scales, notes_words, notes_scales, thr, slope, offs, offs2, offs3, offs4, offs5, offs6):
    idx = unstriped8(offs)
    idx2 = unstriped8(offs2)
    idx3 = unstriped8(offs3)
    idx4 = unstriped8(offs4)
    idx5 = unstriped8(offs5)
    idx6 = unstriped8(offs6)
    keysu = unpack_weight(keys_words, keys_scales, "e4m3")
    notesu = unpack_weight(notes_words, notes_scales, "e2m1")
    queryq = mxq(f64(query), 0, "e4m3")
    a = queryq.T @ keysu
    b = queryq.T @ notesu
    s1 = sigmoid(pick8(b, idx2, 16) * f64(slope) + f64(thr))
    f1 = np.zeros((Q, T))
    f1[np.arange(Q)[:, None], idx3[np.arange(Q) % 128 // 16]] = s1
    aa = a - f1 * 3.0
    w = np.maximum(pick8(aa, idx, 16), pick8(aa, idx4, 16))
    f2 = np.zeros((Q, U))
    f2[np.arange(Q)[:, None], idx5[np.arange(Q) % 128 // 16]] = w
    bb = b + f2
    y = pick8(bb, idx6, 16)
    return y

from contextlib import ExitStack

import concourse.mybir as mybir

D, T, U, SLOTS, Q = 512, 1024, 1024, 512, 128
FLOPS = 2 * D * Q * (T + U)

F32 = mybir.dt.float32
BF16 = mybir.dt.bfloat16
I32 = mybir.dt.int32
U32 = mybir.dt.uint32
U16 = mybir.dt.uint16
U8 = mybir.dt.uint8
FP8X4 = mybir.dt.float8_e4m3fn_x4
FP4X4 = mybir.dt.float4_e2m1fn_x4
ALU = mybir.AluOpType
ACT = mybir.ActivationFunctionType

P = 128
PACK = 4
GROUP = 16
HALF = SLOTS // 2
B_PIECES = (512, 256, 128, 128)
A_PIECE = 512
POOL_SHARE = 256


def load_scale_rows(queue, plane, rows):
    for quad in range(4):
        queue.dma_start(plane[32 * quad : 32 * quad + 4, :].bitcast(I32), rows[0, 4 * quad : 4 * quad + 4, :].bitcast(I32))


def tile_attend_votedown_two_kernel(tc, query, keys_words, keys_scales, notes_words, notes_scales, thr, slope,
                                     offs, offs2, offs3, offs4, offs5, offs6, out):
    nc = tc.nc
    with ExitStack() as ctx:
        lists = ctx.enter_context(tc.tile_pool(name="lists", bufs=1))
        sb = ctx.enter_context(tc.tile_pool(name="sb", bufs=1))
        psum = ctx.enter_context(tc.psum_pool(name="psum", bufs=1))

        def load_list(name, src):
            t = lists.tile([P, SLOTS // GROUP], U16, name=name)
            nc.sync.dma_start(t[:], src)
            return t

        def half(lst, h):
            cols = HALF // GROUP
            return lst[:, h * cols : (h + 1) * cols]

        q_raw = sb.tile([P, PACK, Q], F32, name="q_raw")
        nc.sync.dma_start(q_raw[:], query.rearrange("(p j) q -> p j q", j=PACK))
        n_words = sb.tile([P, 2 * U], U8, name="n_words", align_bytes=64)
        nc.sync.dma_start(n_words[:].bitcast(I32), notes_words[0].bitcast(I32))
        n_plane = sb.tile([P, U], U8, name="n_plane", align_bytes=64)
        load_scale_rows(nc.scalar, n_plane, notes_scales)
        slope_t = sb.tile([P, 1], F32, name="slope_t")
        nc.sync.dma_start(slope_t[:], slope)
        thr_t = sb.tile([P, 1], F32, name="thr_t")
        nc.sync.dma_start(thr_t[:], thr)
        l2 = load_list("l2", offs2)
        l3 = load_list("l3", offs3)
        k_words = sb.tile([P, T], U32, name="k_words", align_bytes=64)
        nc.sync.dma_start(k_words[:].bitcast(I32), keys_words[0].rearrange("p n t -> p (n t)").bitcast(I32))
        k_plane = sb.tile([P, T], U8, name="k_plane", align_bytes=64)
        load_scale_rows(nc.sync, k_plane, keys_scales)
        l1 = load_list("l1", offs)
        l4 = load_list("l4", offs4)
        l5 = load_list("l5", offs5)
        l6 = load_list("l6", offs6)

        warm_in = sb.tile([P, 1], F32, name="warm_in")
        nc.vector.memset(warm_in[:], 0.0)
        warm_out = sb.tile([P, 1], F32, name="warm_out")
        nc.scalar.activation(warm_out[:], warm_in[:], ACT.Sigmoid)

        f1 = sb.tile([P, T], F32, name="f1")
        nc.vector.memset(f1[:], 0.0)
        minus3 = sb.tile([P, HALF], F32, name="minus3")
        nc.vector.memset(minus3[:], -3.0)
        f2 = sb.tile([P, U], F32, name="f2")
        nc.vector.memset(f2[:], 0.0)

        q_bf = sb.tile([P, Q, PACK], BF16, name="q_bf", align_bytes=64)
        nc.vector.tensor_copy(q_bf[:], q_raw[:].rearrange("p j q -> p q j"))
        q_words = sb.tile([P, Q], U32, name="q_words", align_bytes=64)
        q_plane = sb.tile([P, Q], U8, name="q_plane", align_bytes=64)
        nc.vector.quantize_mx(out=q_words[:].bitcast(FP8X4), scales=q_plane[:], in_=q_bf[:].rearrange("p q j -> p (q j)"))

        b = sb.tile([P, U], F32, name="b")
        b_banks = []
        c0 = 0
        for k, width in enumerate(B_PIECES):
            bank = psum.tile([P, width], F32, name="b_bank%d" % k)
            nc.tensor.matmul_mx(out=bank[:], lhsT=q_words[:].bitcast(FP8X4), lhsT_scale=q_plane[:],
                                rhs=n_words[:, 2 * c0 : 2 * (c0 + width)].bitcast(FP4X4),
                                rhs_scale=n_plane[:, c0 : c0 + width], start=True, stop=True)
            if k % 2 == 0:
                nc.vector.tensor_copy(b[:, c0 : c0 + width], bank[:])
            else:
                nc.scalar.copy(b[:, c0 : c0 + width], bank[:])
            b_banks.append((bank, c0, width))
            c0 = c0 + width

        a_banks = []
        for c0 in range(0, T, A_PIECE):
            bank = psum.tile([P, A_PIECE], F32, name="a_bank%d" % c0)
            nc.tensor.matmul_mx(out=bank[:], lhsT=q_words[:].bitcast(FP8X4), lhsT_scale=q_plane[:],
                                rhs=k_words[:, c0 : c0 + A_PIECE].bitcast(FP8X4),
                                rhs_scale=k_plane[:, c0 : c0 + A_PIECE], start=True, stop=True)
            a_banks.append((bank, c0, A_PIECE))
        a_tail = sb.tile([P, POOL_SHARE], F32, name="a_tail")
        nc.scalar.copy(a_tail[:], a_banks[-1][0][:, A_PIECE - POOL_SHARE :])

        def add_dense(dst, banks, tail, field):
            split = T - POOL_SHARE
            nc.gpsimd.tensor_tensor(dst[:, split:], tail, field[:, split:], ALU.add)
            for bank, c0, width in banks:
                n = min(width, split - c0)
                if n > 0:
                    nc.vector.tensor_tensor(dst[:, c0 : c0 + n], bank[:, 0:n], field[:, c0 : c0 + n], ALU.add)

        for h in range(2):
            s1 = sb.tile([P, HALF], F32, name="s1_%d" % h)
            nc.scalar.activation(s1[:], b[:].indirect(half(l2, h)), ACT.Sigmoid, bias=thr_t[:], scale=slope_t[:])
            nc.vector.tensor_tensor(f1[:].indirect(half(l3, h)), s1[:], minus3[:], ALU.mult)

        aa = sb.tile([P, T], F32, name="aa")
        add_dense(aa, a_banks, a_tail[:], f1)

        g1 = [sb.tile([P, HALF], F32, name="g1_%d" % h) for h in range(2)]
        g4 = [sb.tile([P, HALF], F32, name="g4_%d" % h) for h in range(2)]
        nc.vector.tensor_copy(g1[0][:], aa[:].indirect(half(l1, 0)))
        nc.scalar.activation(g4[0][:], aa[:].indirect(half(l4, 0)), ACT.Copy)
        nc.scalar.activation(g4[1][:], aa[:].indirect(half(l4, 1)), ACT.Copy)
        nc.scalar.activation(g1[1][:], aa[:].indirect(half(l1, 1)), ACT.Copy)
        w = sb.tile([P, SLOTS], F32, name="w")
        lead = 128
        nc.vector.tensor_tensor(w[:, 0:lead], g1[0][:, 0:lead], g4[0][:, 0:lead], ALU.max)
        nc.vector.tensor_tensor(w[:, lead:HALF], g1[0][:, lead:HALF], g4[0][:, lead:HALF], ALU.max)
        nc.vector.tensor_copy(f2[:].indirect(l5[:, 0 : lead // GROUP]), w[:, 0:lead])
        nc.vector.tensor_tensor(w[:, HALF:SLOTS], g1[1][:], g4[1][:], ALU.max)
        nc.vector.tensor_copy(f2[:].indirect(l5[:, lead // GROUP :]), w[:, lead:SLOTS])

        bb = sb.tile([P, U], F32, name="bb")
        add_dense(bb, b_banks, b[:, U - POOL_SHARE :], f2)

        y0 = sb.tile([P, HALF], F32, name="y0")
        nc.vector.tensor_copy(y0[:], bb[:].indirect(half(l6, 0)))
        nc.sync.dma_start(out[:, 0:HALF], y0[:])
        y1 = sb.tile([P, HALF], F32, name="y1")
        nc.scalar.activation(y1[:], bb[:].indirect(half(l6, 1)), ACT.Copy)
        nc.scalar.dma_start(out[:, HALF:SLOTS], y1[:])
